import numpy as np
import ml_dtypes


def mxq(x, axis, fmt="e4m3"):
    dtype, down = {"e4m3": (ml_dtypes.float8_e4m3fn, 7), "e5m2": (ml_dtypes.float8_e5m2, 14)}[fmt]
    v = np.moveaxis(np.asarray(x, np.float32).astype(ml_dtypes.bfloat16).astype(np.float64), axis, -1)
    blocks = v.reshape(v.shape[:-1] + (-1, 32))
    amax = np.abs(blocks).max(-1, keepdims=True)
    byte = np.maximum(np.where(amax > 0, np.frexp(amax)[1] - 1 + 127, 0) - down, 1)
    scale = np.exp2(byte - 127.0)
    codes = (blocks / scale).astype(np.float32).astype(dtype).astype(np.float64)
    return np.moveaxis((codes * scale).reshape(v.shape), -1, axis)


WIDE = False


def mx_kscale(k):
    if not WIDE:
        return np.ones(k)
    levels = np.array([10, -10, 5, -5, 0])
    if k % 512:
        return np.exp2(np.random.permutation(np.resize(levels, k // 32))).repeat(32)
    a = np.empty((k // 512, 16))
    for p in range(k // 512):
        a[p, :8] = np.random.permutation(np.resize(levels, 8))
        for g in range(8):
            far = levels[np.abs(levels - a[p, g]) >= 10]
            a[p, g + 8] = far[np.random.randint(len(far))]
    return np.exp2(a.ravel()).repeat(32)


def f64(x):
    return np.asarray(x).astype(np.float64)


def striped(idx):
    return np.tile(idx.reshape(-1, 16).T, (8, 1)).astype(np.uint16)


def unstriped(offs):
    return offs[:16].T.reshape(-1).astype(np.int64)


def striped8(idx):
    return np.concatenate([x.reshape(-1, 16).T for x in idx]).astype(np.uint16)


def runs(offs, k):
    lists = np.stack([offs[16 * r : 16 * r + 16].T.reshape(-1) for r in range(8)]).astype(np.int64)
    return lists[np.arange(k) % 512 // 64]


def pack_weight(w):
    k, n = w.shape
    w = f64(np.asarray(w, np.float32).astype(ml_dtypes.bfloat16)).reshape(k // 32, 32, n)
    amax = np.abs(w).max(1)
    byte = np.clip(np.where(amax > 0, np.frexp(amax)[1] - 1 + 127 - 7, 1), 1, 254)
    scaled = (w * np.exp2(127.0 - byte)[:, None, :]).reshape(k, n).astype(np.float32)
    words = np.ascontiguousarray(scaled.reshape(k // 512, 128, 4, n).transpose(0, 1, 3, 2)).astype(ml_dtypes.float8_e4m3fn).view(np.uint8)
    return words, np.ascontiguousarray(byte.astype(np.uint8).reshape(k // 512, 16, n))


def unpack_weight(words, scales):
    g, p, n, _ = words.shape
    vals = np.ascontiguousarray(words).view(ml_dtypes.float8_e4m3fn).astype(np.float64) * np.repeat(np.exp2(scales.astype(np.float64) - 127.0), 8, axis=1)[..., None]
    return vals.transpose(0, 1, 3, 2).reshape(g * 512, n)


K, T, S, N, H = 512, 2048, 256, 512, 512


def setup_inputs():
    n = np.random.standard_normal
    s = mx_kscale(K)[:, None]
    u = mx_kscale(H)
    packed_xT = pack_weight(n((K, T)) * s)
    return {
        "x_words": packed_xT[0],
        "x_scales": packed_xT[1],
        "w1": (n((K, H)) / np.sqrt(K) / s).astype(np.float32),
        "w2": (n((K, H)) / np.sqrt(K) / s).astype(np.float32),
        "tau": np.random.uniform(0.3, 0.9, (H, 1)).astype(np.float32),
        "gn": (np.random.uniform(0.5, 1.5, (H, 1)) * u[:, None]).astype(np.float32),
        "gm": (np.random.uniform(0.5, 1.5, (H, 1)) * u[:, None]).astype(np.float32),
        "w3": (n((H, N)) / np.sqrt(2 * H) / u[:, None]).astype(np.float32),
        "w4": (n((H, N)) / np.sqrt(2 * H) / u[:, None]).astype(np.float32),
        "tau2": np.random.uniform(0.3, 0.9, (N, 1)).astype(np.float32),
        "offs": striped(np.random.permutation(T)[:S]),
        "hz": striped8(np.random.randint(0, T, (8, S))),
        "n1": striped(np.random.permutation(S)),
        "n2": striped(np.random.permutation(S)),
        "n3": striped(np.random.permutation(S)),
        "n4": striped(np.random.permutation(S)),
        "n5": striped(np.random.permutation(S)),
        "n6": striped(np.random.permutation(S)),
    }


def reference(x_words, x_scales, w1, w2, tau, gn, gm, w3, w4, tau2, offs, hz, n1, n2, n3, n4, n5, n6):
    xq = unpack_weight(x_words, x_scales)[:, unstriped(offs)]
    y = mxq(f64(w1), 0, "e4m3").T @ xq
    st = y - y[:, unstriped(n1)]
    su = np.maximum(st, st[:, unstriped(n2)])
    z = f64(gn) * (su + 0.5 * su[:, unstriped(n3)])
    x_hz = unpack_weight(x_words, x_scales)[np.arange(K)[:, None], runs(hz, K)]
    d = mxq(f64(w2), 0, "e4m3").T @ x_hz
    top = d.max(axis=1, keepdims=True)
    ea = np.exp(f64(tau) * (d[:, unstriped(n4)] - top))
    z2 = f64(gm) * (2.0 * (d * ea))
    h = mxq(f64(w3), 0, "e4m3").T @ mxq(z, 0, "e4m3") + mxq(f64(w4), 0, "e4m3").T @ mxq(z2, 0, "e4m3")
    top2 = h.max(axis=1, keepdims=True)
    ea2 = np.exp(f64(tau2) * (h[:, unstriped(n5)] - top2))
    return np.maximum(h, 2.0 * ea2) - (0.5 * h[:, unstriped(n6)])

@@ -1,0 +1,260 @@
+from contextlib import ExitStack
+
+import concourse.mybir as mybir
+
+F32 = mybir.dt.float32
+BF16 = mybir.dt.bfloat16
+I32 = mybir.dt.int32
+U32 = mybir.dt.uint32
+U16 = mybir.dt.uint16
+U8 = mybir.dt.uint8
+FP8X4 = mybir.dt.float8_e4m3fn_x4
+ALU = mybir.AluOpType
+ACT = mybir.ActivationFunctionType
+
+P = 128
+PACK = 4
+T = 2048
+S = 256
+H = 512
+WIN = 2 * S
+
+FLOPS = 2 * 4 * 512 * 512 * 256
+
+
+def tile_picked_hjointhreeepkecl_none_p_kernel(
+    tc, x_words, x_scales, w1, w2, tau, gn, gm, w3, w4, tau2, offs, hz, n1, n2, n3, n4, n5, n6, out
+):
+    nc = tc.nc
+    with ExitStack() as ctx:
+        keep = ctx.enter_context(tc.tile_pool(name="keep", bufs=1))
+        psum = ctx.enter_context(tc.psum_pool(name="psum", bufs=1))
+
+        def load_list(src, name):
+            lst = keep.tile([P, S // 16], U16, name=name)
+            nc.sync.dma_start(lst[:], src)
+            return lst
+
+        def load_rows(src, name):
+            vec = keep.tile([P, PACK], F32, name=name)
+            nc.gpsimd.dma_start(vec[:], src.rearrange("(p t) o -> p (t o)", t=PACK))
+            return vec
+
+        def load_weight(src, name, tag):
+            raw = keep.tile([P, PACK, H], F32, name=name, tag=tag)
+            nc.sync.dma_start(raw[:], src.rearrange("(p j) c -> p j c", j=PACK))
+            return raw
+
+        def weight_tiles(name):
+            return (
+                keep.tile([P, PACK * H], BF16, name=name + "_bf", align_bytes=64),
+                keep.tile([P, H], U32, name=name + "_codes", align_bytes=64),
+                keep.tile([P, H], U8, name=name + "_scales", align_bytes=64),
+            )
+
+        def round_copy(engine, dst, src):
+            if engine == "scalar":
+                nc.scalar.activation(dst, src, ACT.Copy)
+            else:
+                nc.vector.tensor_copy(dst, src)
+
+        def cast_dealt(engine, wt, raw, raw_c0, c0, c1):
+            dst = wt[0][:].rearrange("p (t m j) -> p m j t", t=PACK, j=PACK)[:, c0 // PACK : c1 // PACK]
+            src = raw[:, :, c0 - raw_c0 : c1 - raw_c0].rearrange("p j (m t) -> p m j t", t=PACK)
+            round_copy(engine, dst, src)
+
+        def cast_plain(engine, wt, raw, t):
+            dst = wt[0][:, PACK * P * t : PACK * P * (t + 1)].rearrange("p (c i j) -> p c j i", i=4, j=PACK)
+            src = raw[:, :, P * t : P * (t + 1)].rearrange("p j (c i) -> p c j i", i=4)
+            round_copy(engine, dst, src)
+
+        def quantize(wt, t0, t1):
+            cols = slice(P * t0, P * t1)
+            nc.vector.quantize_mx(
+                out=wt[1][:, cols].bitcast(FP8X4), scales=wt[2][:, cols], in_=wt[0][:, PACK * P * t0 : PACK * P * t1]
+            )
+
+        def product(bank, wt, t, codes, scales, start, stop):
+            cols = slice(P * t, P * (t + 1))
+            nc.tensor.matmul_mx(
+                out=bank[:], lhsT=wt[1][:, cols].bitcast(FP8X4), lhsT_scale=wt[2][:, cols],
+                rhs=codes[:].bitcast(FP8X4), rhs_scale=scales[:], start=start, stop=stop,
+            )
+
+        def planes(name):
+            tile = keep.tile([P, (PACK + 1) * S], F32, name=name)
+            nc.vector.memset(tile[:, PACK * S :], 0.0)
+            return tile
+
+        def window(name):
+            tile = keep.tile([P, WIN], F32, name=name)
+            nc.vector.memset(tile[:, S:], 0.0)
+            return tile
+
+        def plane(tile, t):
+            return tile[:, S * t : S * (t + 1)]
+
+        def plane_window(tile, t):
+            return tile[:, S * t : S * t + WIN]
+
+        def woven(tile):
+            return tile[:, : PACK * S].rearrange("p (t c i) -> p c t i", t=PACK, i=4)
+
+        order = [3, 2, 1, 0]
+
+        scale_table = keep.tile([P, T], U8, name="scale_table")
+        nc.gpsimd.memset(scale_table[:].bitcast(I32), 0)
+        scale_rows = x_scales[0].bitcast(I32)
+        offs_t = load_list(offs, "offs_t")
+        hz_t = load_list(hz, "hz_t")
+        n1_t = load_list(n1, "n1_t")
+        n2_t = load_list(n2, "n2_t")
+        n3_t = load_list(n3, "n3_t")
+        w1_raw = load_weight(w1, "w1_raw", "raw_a")
+        n4_t = load_list(n4, "n4_t")
+        n5_t = load_list(n5, "n5_t")
+        for r in (0, 1):
+            nc.sync.dma_start(scale_table[r:P:16, :].bitcast(I32), scale_rows[r:16:2, :])
+        for r in (2, 3):
+            nc.sync.dma_start(scale_table[r:P:32, :].bitcast(I32), scale_rows[r:16:4, :])
+        word_table = keep.tile([P, T], I32, name="word_table")
+        nc.sync.dma_start(word_table[:], x_words[0].rearrange("p n t -> p (n t)").bitcast(I32))
+        w2_raw = load_weight(w2, "w2_raw", "raw_b")
+        n6_t = load_list(n6, "n6_t")
+
+        xo_scales = keep.tile([P, S], U8, name="xo_scales", align_bytes=64)
+        xh_gathered = keep.tile([P, S], U8, name="xh_gathered", align_bytes=64)
+        xh_scales = keep.tile([P, S], U8, name="xh_scales", align_bytes=64)
+        xo_words = keep.tile([P, S], U32, name="xo_words", align_bytes=64)
+        xh_words = keep.tile([P, S], U32, name="xh_words", align_bytes=64)
+        nc.vector.tensor_copy(xh_gathered[:], scale_table[:].indirect(hz_t[:]))
+        nc.vector.tensor_copy(xh_scales[:].bitcast(I32), xh_gathered[:].bitcast(I32))
+        nc.vector.tensor_copy(xo_scales[:], scale_table[:].indirect(offs_t[:]))
+        for r in (2, 3):
+            nc.sync.dma_start(xh_scales[r:P:32, :].bitcast(I32), xh_gathered[14 + r : P : 32, :].bitcast(I32))
+
+        tau_t = load_rows(tau, "tau_t")
+        gn_t = load_rows(gn, "gn_t")
+        gm_t = load_rows(gm, "gm_t")
+        tau2_t = keep.tile([P, PACK], F32, name="tau2_t")
+        with nc.allow_non_contiguous_dma(reason="one rate a row: 512 values in all"):
+            nc.gpsimd.dma_start(tau2_t[:], tau2.rearrange("(t p) o -> p (t o)", p=P))
+
+        y_pl = planes("y_pl")
+        st_pl = planes("st_pl")
+        u_pl = planes("u_pl")
+        d_win = [window("d_win%d" % t) for t in range(PACK)]
+        h_win = [window("h_win%d" % t) for t in range(PACK)]
+
+        wt1, wt2, wt3, wt4 = [weight_tiles(n) for n in ("w1", "w2", "w3", "w4")]
+        cast_dealt("scalar", wt1, w1_raw, 0, 0, 320)
+        cast_dealt("vector", wt1, w1_raw, 0, 320, H)
+        w3_raw = load_weight(w3, "w3_raw", "raw_a")
+
+        quantize(wt1, 0, PACK)
+        nc.vector.tensor_copy(xo_words[:], word_table[:].bitcast(U32).indirect(offs_t[:]))
+
+        y_bank = {}
+        for t in order:
+            y_bank[t] = psum.tile([P, S], F32, name="y_bank%d" % t, tag="a%d" % t)
+            product(y_bank[t], wt1, t, xo_words, xo_scales, True, True)
+
+        nc.vector.tensor_copy(xh_words[:], word_table[:].bitcast(U32).indirect(hz_t[:]))
+
+        for h in range(2):
+            cast_dealt("vector", wt2, w2_raw, 0, 256 * h, 256 * (h + 1))
+        w4_raw = load_weight(w4, "w4_raw", "raw_b")
+        quantize(wt2, 0, PACK)
+        d_bank = {}
+        for t in order:
+            d_bank[t] = psum.tile([P, S], F32, name="d_bank%d" % t, tag="b%d" % t)
+            product(d_bank[t], wt2, t, xh_words, xh_scales, True, True)
+
+        g1 = keep.tile([P, PACK * S], F32, name="g1")
+        g2 = keep.tile([P, PACK * S], F32, name="g2")
+        g3 = keep.tile([P, PACK * S], F32, name="g3")
+        su = keep.tile([P, PACK * S], F32, name="su")
+        for t in order:
+            nc.scalar.copy(plane(y_pl, t), y_bank[t][:])
+            nc.scalar.activation(plane(g1, t), plane_window(y_pl, t).indirect(n1_t[:]), ACT.Copy)
+            nc.vector.tensor_tensor(plane(st_pl, t), y_bank[t][:], plane(g1, t), ALU.subtract)
+
+        top = keep.tile([P, PACK], F32, name="top")
+        bias = keep.tile([P, PACK], F32, name="bias")
+        ea = keep.tile([P, PACK * S], F32, name="ea")
+        dg = keep.tile([P, PACK * S], F32, name="dg")
+        for t in order:
+            col = slice(t, t + 1)
+            nc.scalar.activation(plane(g2, t), plane_window(st_pl, t).indirect(n2_t[:]), ACT.Copy)
+            nc.vector.tensor_tensor(plane(su, t), plane(st_pl, t), plane(g2, t), ALU.max)
+            nc.vector.tensor_scalar(plane(u_pl, t), plane(su, t), gn_t[:, col], None, ALU.mult)
+        for t in order:
+            col = slice(t, t + 1)
+            nc.vector.tensor_scalar(d_win[t][:, :S], d_bank[t][:], 1.0, None, ALU.mult, ALU.max, accum_out=top[:, col])
+            nc.gpsimd.tensor_scalar(bias[:, col], top[:, col], tau_t[:, col], -1.0, ALU.mult, ALU.mult)
+            nc.vector.tensor_scalar(plane(dg, t), d_win[t][:, :S], gm_t[:, col], 2.0, ALU.mult, ALU.mult)
+
+        for t in order:
+            cast_plain("vector", wt3, w3_raw, t)
+        quantize(wt3, 0, PACK)
+
+        z2_bf = keep.tile([P, PACK * S], BF16, name="z2_bf", align_bytes=64)
+        z2_codes = keep.tile([P, S], U32, name="z2_codes", align_bytes=64)
+        z2_scales = keep.tile([P, S], U8, name="z2_scales", align_bytes=64)
+        z_bf = keep.tile([P, PACK * S], BF16, name="z_bf", align_bytes=64)
+        z_codes = keep.tile([P, S], U32, name="z_codes", align_bytes=64)
+        z_scales = keep.tile([P, S], U8, name="z_scales", align_bytes=64)
+
+        def packed(tile):
+            return tile[:].rearrange("p (c i t) -> p c t i", t=PACK, i=4)
+
+        for t in order:
+            nc.scalar.activation(plane(g3, t), plane_window(u_pl, t).indirect(n3_t[:]), ACT.Copy, scale=0.5)
+        for t in order:
+            col = slice(t, t + 1)
+            nc.scalar.activation(plane(ea, t), d_win[t][:].indirect(n4_t[:]), ACT.Exp, bias=bias[:, col], scale=tau_t[:, col])
+        nc.vector.tensor_tensor(packed(z_bf), woven(u_pl), woven(g3), ALU.add)
+        nc.vector.quantize_mx(out=z_codes[:].bitcast(FP8X4), scales=z_scales[:], in_=z_bf[:])
+        h_bank = {}
+        for t in order:
+            h_bank[t] = psum.tile([P, S], F32, name="h_bank%d" % t, tag="a%d" % t)
+            product(h_bank[t], wt3, t, z_codes, z_scales, True, False)
+        nc.vector.tensor_tensor(packed(z2_bf), woven(dg), woven(ea), ALU.mult)
+        nc.vector.quantize_mx(out=z2_codes[:].bitcast(FP8X4), scales=z2_scales[:], in_=z2_bf[:])
+
+        top2 = keep.tile([P, PACK], F32, name="top2")
+        bias2 = keep.tile([P, PACK], F32, name="bias2")
+        ea2 = [keep.tile([P, S], F32, name="ea2_%d" % t) for t in range(PACK)]
+        g6 = [keep.tile([P, S], F32, name="g6_%d" % t) for t in range(PACK)]
+        for t in order:
+            col = slice(t, t + 1)
+            cast_plain("scalar", wt4, w4_raw, t)
+            quantize(wt4, t, t + 1)
+            product(h_bank[t], wt4, t, z2_codes, z2_scales, False, True)
+            nc.vector.tensor_scalar(h_win[t][:, :S], h_bank[t][:], 1.0, None, ALU.mult, ALU.max, accum_out=top2[:, col])
+            nc.gpsimd.tensor_scalar(bias2[:, col], top2[:, col], tau2_t[:, col], -1.0, ALU.mult, ALU.mult)
+
+        def fetch(t):
+            nc.scalar.activation(g6[t][:], h_win[t][:].indirect(n6_t[:]), ACT.Copy)
+
+        def expo(t):
+            col = slice(t, t + 1)
+            nc.scalar.activation(ea2[t][:], h_win[t][:].indirect(n5_t[:]), ACT.Exp, bias=bias2[:, col], scale=tau2_t[:, col])
+
+        def finish(t):
+            big = keep.tile([P, S], F32, name="big_%d" % t)
+            res = keep.tile([P, S], F32, name="res_%d" % t)
+            nc.vector.scalar_tensor_tensor(big[:], ea2[t][:], 2.0, h_bank[t][:], ALU.mult, ALU.max)
+            nc.vector.scalar_tensor_tensor(res[:], g6[t][:], -0.5, big[:], ALU.mult, ALU.add)
+            nc.sync.dma_start(out[P * t : P * (t + 1), :], res[:])
+
+        nc.vector.tensor_copy(g6[0][:], h_win[0][:].indirect(n6_t[:]))
+        fetch(3)
+        expo(3)
+        expo(2)
+        fetch(2)
+        expo(1)
+        expo(0)
+        fetch(1)
+        for t in (3, 2, 0, 1):
+            finish(t)

@@ -17,7 +17,12 @@ PACK = 4
 T = 2048
 S = 256
 H = 512
+HALF = H // 2
 WIN = 2 * S
+LINE = 4
+GROUP = 16
+QUAD = 32
+BLOCK_ROWS = 8
 
 FLOPS = 2 * 4 * 512 * 512 * 256
 
@@ -31,62 +36,55 @@ def tile_picked_hjointhreeepkecl_none_p_kernel(
         psum = ctx.enter_context(tc.psum_pool(name="psum", bufs=1))
 
         def load_list(src, name):
-            lst = keep.tile([P, S // 16], U16, name=name)
+            lst = keep.tile([P, S // GROUP], U16, name=name)
             nc.sync.dma_start(lst[:], src)
             return lst
 
-        def load_rows(src, name):
+        def load_dealt_rows(src, name):
             vec = keep.tile([P, PACK], F32, name=name)
-            nc.gpsimd.dma_start(vec[:], src.rearrange("(p t) o -> p (t o)", t=PACK))
+            nc.sync.dma_start(vec[:], src.rearrange("(p t) o -> p (t o)", t=PACK))
             return vec
 
-        def load_weight(src, name, tag):
-            raw = keep.tile([P, PACK, H], F32, name=name, tag=tag)
-            nc.sync.dma_start(raw[:], src.rearrange("(p j) c -> p j c", j=PACK))
-            return raw
+        def load_columns(raw, src, c0, c1):
+            nc.sync.dma_start(raw[:, :, c0:c1], src.rearrange("(p j) c -> p j c", j=PACK)[:, :, c0:c1])
 
-        def weight_tiles(name):
+        def operand(name, width, tag, codes_tag):
             return (
-                keep.tile([P, PACK * H], BF16, name=name + "_bf", align_bytes=64),
-                keep.tile([P, H], U32, name=name + "_codes", align_bytes=64),
-                keep.tile([P, H], U8, name=name + "_scales", align_bytes=64),
+                keep.tile([P, PACK * width], BF16, name=name + "_bf", tag=tag, align_bytes=64),
+                keep.tile([P, width], U32, name=name + "_codes", tag=codes_tag, align_bytes=64),
+                keep.tile([P, width], U8, name=name + "_scales", align_bytes=64),
             )
 
-        def round_copy(engine, dst, src):
-            if engine == "scalar":
-                nc.scalar.activation(dst, src, ACT.Copy)
-            else:
-                nc.vector.tensor_copy(dst, src)
+        def round_on_vector(dst, src):
+            nc.vector.tensor_copy(dst, src)
 
-        def cast_dealt(engine, wt, raw, raw_c0, c0, c1):
-            dst = wt[0][:].rearrange("p (t m j) -> p m j t", t=PACK, j=PACK)[:, c0 // PACK : c1 // PACK]
-            src = raw[:, :, c0 - raw_c0 : c1 - raw_c0].rearrange("p j (m t) -> p m j t", t=PACK)
-            round_copy(engine, dst, src)
+        def round_on_scalar(dst, src):
+            nc.scalar.activation(dst, src, ACT.Copy)
 
-        def cast_plain(engine, wt, raw, t):
-            dst = wt[0][:, PACK * P * t : PACK * P * (t + 1)].rearrange("p (c i j) -> p c j i", i=4, j=PACK)
-            src = raw[:, :, P * t : P * (t + 1)].rearrange("p j (c i) -> p c j i", i=4)
-            round_copy(engine, dst, src)
+        def round_dealt(rounder, op, raw, c0, c1):
+            dst = op[0][:].rearrange("p (t m j) -> p m j t", t=PACK, j=PACK)[:, c0 // PACK : c1 // PACK]
+            rounder(dst, raw[:, :, c0:c1].rearrange("p j (m t) -> p m j t", t=PACK))
 
-        def quantize(wt, t0, t1):
-            cols = slice(P * t0, P * t1)
-            nc.vector.quantize_mx(
-                out=wt[1][:, cols].bitcast(FP8X4), scales=wt[2][:, cols], in_=wt[0][:, PACK * P * t0 : PACK * P * t1]
-            )
+        def round_block(rounder, op, b, raw, t):
+            dst = op[0][:, PACK * P * b : PACK * P * (b + 1)].rearrange("p (c a j) -> p c j a", a=LINE, j=PACK)
+            rounder(dst, raw[:, :, P * t : P * (t + 1)].rearrange("p j (c a) -> p c j a", a=LINE))
 
-        def product(bank, wt, t, codes, scales, start, stop):
-            cols = slice(P * t, P * (t + 1))
+        def quantize(op):
+            nc.vector.quantize_mx(out=op[1][:].bitcast(FP8X4), scales=op[2][:], in_=op[0][:])
+
+        def product(bank, op, b, codes, scales, start, stop):
+            cols = slice(P * b, P * (b + 1))
             nc.tensor.matmul_mx(
-                out=bank[:], lhsT=wt[1][:, cols].bitcast(FP8X4), lhsT_scale=wt[2][:, cols],
-                rhs=codes[:].bitcast(FP8X4), rhs_scale=scales[:], start=start, stop=stop,
+                out=bank[:], lhsT=op[1][:, cols].bitcast(FP8X4), lhsT_scale=op[2][:, cols],
+                rhs=codes.bitcast(FP8X4), rhs_scale=scales, start=start, stop=stop,
             )
 
-        def planes(name):
-            tile = keep.tile([P, (PACK + 1) * S], F32, name=name)
+        def planes_with_spare(name, tag):
+            tile = keep.tile([P, (PACK + 1) * S], F32, name=name, tag=tag)
             nc.vector.memset(tile[:, PACK * S :], 0.0)
             return tile
 
-        def window(name):
+        def window_tile(name):
             tile = keep.tile([P, WIN], F32, name=name)
             nc.vector.memset(tile[:, S:], 0.0)
             return tile
@@ -98,163 +96,183 @@ def tile_picked_hjointhreeepkecl_none_p_kernel(
             return tile[:, S * t : S * t + WIN]
 
         def woven(tile):
-            return tile[:, : PACK * S].rearrange("p (t c i) -> p c t i", t=PACK, i=4)
-
-        order = [3, 2, 1, 0]
-
-        scale_table = keep.tile([P, T], U8, name="scale_table")
-        nc.gpsimd.memset(scale_table[:].bitcast(I32), 0)
-        scale_rows = x_scales[0].bitcast(I32)
-        offs_t = load_list(offs, "offs_t")
-        hz_t = load_list(hz, "hz_t")
-        n1_t = load_list(n1, "n1_t")
-        n2_t = load_list(n2, "n2_t")
-        n3_t = load_list(n3, "n3_t")
-        w1_raw = load_weight(w1, "w1_raw", "raw_a")
-        n4_t = load_list(n4, "n4_t")
-        n5_t = load_list(n5, "n5_t")
-        for r in (0, 1):
-            nc.sync.dma_start(scale_table[r:P:16, :].bitcast(I32), scale_rows[r:16:2, :])
-        for r in (2, 3):
-            nc.sync.dma_start(scale_table[r:P:32, :].bitcast(I32), scale_rows[r:16:4, :])
-        word_table = keep.tile([P, T], I32, name="word_table")
-        nc.sync.dma_start(word_table[:], x_words[0].rearrange("p n t -> p (n t)").bitcast(I32))
-        w2_raw = load_weight(w2, "w2_raw", "raw_b")
-        n6_t = load_list(n6, "n6_t")
-
-        xo_scales = keep.tile([P, S], U8, name="xo_scales", align_bytes=64)
-        xh_gathered = keep.tile([P, S], U8, name="xh_gathered", align_bytes=64)
-        xh_scales = keep.tile([P, S], U8, name="xh_scales", align_bytes=64)
-        xo_words = keep.tile([P, S], U32, name="xo_words", align_bytes=64)
-        xh_words = keep.tile([P, S], U32, name="xh_words", align_bytes=64)
-        nc.vector.tensor_copy(xh_gathered[:], scale_table[:].indirect(hz_t[:]))
-        nc.vector.tensor_copy(xh_scales[:].bitcast(I32), xh_gathered[:].bitcast(I32))
-        nc.vector.tensor_copy(xo_scales[:], scale_table[:].indirect(offs_t[:]))
-        for r in (2, 3):
-            nc.sync.dma_start(xh_scales[r:P:32, :].bitcast(I32), xh_gathered[14 + r : P : 32, :].bitcast(I32))
-
-        tau_t = load_rows(tau, "tau_t")
-        gn_t = load_rows(gn, "gn_t")
-        gm_t = load_rows(gm, "gm_t")
-        tau2_t = keep.tile([P, PACK], F32, name="tau2_t")
-        with nc.allow_non_contiguous_dma(reason="one rate a row: 512 values in all"):
-            nc.gpsimd.dma_start(tau2_t[:], tau2.rearrange("(t p) o -> p (t o)", p=P))
-
-        y_pl = planes("y_pl")
-        st_pl = planes("st_pl")
-        u_pl = planes("u_pl")
-        d_win = [window("d_win%d" % t) for t in range(PACK)]
-        h_win = [window("h_win%d" % t) for t in range(PACK)]
-
-        wt1, wt2, wt3, wt4 = [weight_tiles(n) for n in ("w1", "w2", "w3", "w4")]
-        cast_dealt("scalar", wt1, w1_raw, 0, 0, 320)
-        cast_dealt("vector", wt1, w1_raw, 0, 320, H)
-        w3_raw = load_weight(w3, "w3_raw", "raw_a")
-
-        quantize(wt1, 0, PACK)
-        nc.vector.tensor_copy(xo_words[:], word_table[:].bitcast(U32).indirect(offs_t[:]))
-
-        y_bank = {}
-        for t in order:
-            y_bank[t] = psum.tile([P, S], F32, name="y_bank%d" % t, tag="a%d" % t)
-            product(y_bank[t], wt1, t, xo_words, xo_scales, True, True)
-
-        nc.vector.tensor_copy(xh_words[:], word_table[:].bitcast(U32).indirect(hz_t[:]))
-
-        for h in range(2):
-            cast_dealt("vector", wt2, w2_raw, 0, 256 * h, 256 * (h + 1))
-        w4_raw = load_weight(w4, "w4_raw", "raw_b")
-        quantize(wt2, 0, PACK)
-        d_bank = {}
-        for t in order:
-            d_bank[t] = psum.tile([P, S], F32, name="d_bank%d" % t, tag="b%d" % t)
-            product(d_bank[t], wt2, t, xh_words, xh_scales, True, True)
-
-        g1 = keep.tile([P, PACK * S], F32, name="g1")
-        g2 = keep.tile([P, PACK * S], F32, name="g2")
-        g3 = keep.tile([P, PACK * S], F32, name="g3")
-        su = keep.tile([P, PACK * S], F32, name="su")
-        for t in order:
-            nc.scalar.copy(plane(y_pl, t), y_bank[t][:])
-            nc.scalar.activation(plane(g1, t), plane_window(y_pl, t).indirect(n1_t[:]), ACT.Copy)
-            nc.vector.tensor_tensor(plane(st_pl, t), y_bank[t][:], plane(g1, t), ALU.subtract)
-
-        top = keep.tile([P, PACK], F32, name="top")
-        bias = keep.tile([P, PACK], F32, name="bias")
-        ea = keep.tile([P, PACK * S], F32, name="ea")
-        dg = keep.tile([P, PACK * S], F32, name="dg")
-        for t in order:
-            col = slice(t, t + 1)
-            nc.scalar.activation(plane(g2, t), plane_window(st_pl, t).indirect(n2_t[:]), ACT.Copy)
-            nc.vector.tensor_tensor(plane(su, t), plane(st_pl, t), plane(g2, t), ALU.max)
-            nc.vector.tensor_scalar(plane(u_pl, t), plane(su, t), gn_t[:, col], None, ALU.mult)
-        for t in order:
-            col = slice(t, t + 1)
-            nc.vector.tensor_scalar(d_win[t][:, :S], d_bank[t][:], 1.0, None, ALU.mult, ALU.max, accum_out=top[:, col])
-            nc.gpsimd.tensor_scalar(bias[:, col], top[:, col], tau_t[:, col], -1.0, ALU.mult, ALU.mult)
-            nc.vector.tensor_scalar(plane(dg, t), d_win[t][:, :S], gm_t[:, col], 2.0, ALU.mult, ALU.mult)
-
-        for t in order:
-            cast_plain("vector", wt3, w3_raw, t)
-        quantize(wt3, 0, PACK)
-
-        z2_bf = keep.tile([P, PACK * S], BF16, name="z2_bf", align_bytes=64)
-        z2_codes = keep.tile([P, S], U32, name="z2_codes", align_bytes=64)
-        z2_scales = keep.tile([P, S], U8, name="z2_scales", align_bytes=64)
-        z_bf = keep.tile([P, PACK * S], BF16, name="z_bf", align_bytes=64)
-        z_codes = keep.tile([P, S], U32, name="z_codes", align_bytes=64)
-        z_scales = keep.tile([P, S], U8, name="z_scales", align_bytes=64)
+            return tile[:, : PACK * S].rearrange("p (t c a) -> p c t a", t=PACK, a=LINE)
 
         def packed(tile):
-            return tile[:].rearrange("p (c i t) -> p c t i", t=PACK, i=4)
+            return tile[:].rearrange("p (c a t) -> p c t a", t=PACK, a=LINE)
+
+        order = list(reversed(range(PACK)))
+
+        scale_table = keep.tile([P, T], U8, name="scale_table", tag="raw_b")
+        nc.gpsimd.memset(scale_table[:].bitcast(I32), 0)
+        w1_raw = keep.tile([P, PACK, H], F32, name="w1_raw", tag="raw_a")
+        load_columns(w1_raw, w1, 0, HALF)
+        offs_t = load_list(offs, "offs_t")
+        hz_t = load_list(hz, "hz_t")
+        nc.sync.dma_start(scale_table[0:P:BLOCK_ROWS, :].bitcast(I32), x_scales[0].bitcast(I32))
+        load_columns(w1_raw, w1, HALF, H)
+        word_table = keep.tile([P, T], I32, name="word_table", tag="raw_c")
+        nc.sync.dma_start(word_table[:], x_words[0].rearrange("p c j -> p (c j)").bitcast(I32))
+
+        picked_scales = keep.tile([P, 2 * S], U8, name="picked_scales")
+        x_scale_rows = keep.tile([P, 2 * S], U8, name="x_scale_rows", align_bytes=64)
+        nc.vector.memset(x_scale_rows[:].bitcast(I32), 0)
+        nc.vector.tensor_copy(picked_scales[:, :S], scale_table[:].indirect(offs_t[:]))
+        nc.vector.tensor_copy(picked_scales[:, S:], scale_table[:].indirect(hz_t[:]))
+        for q0 in range(0, P, QUAD):
+            nc.sync.dma_start(
+                x_scale_rows[q0 : q0 + QUAD // BLOCK_ROWS, :].bitcast(I32),
+                picked_scales[q0 : q0 + QUAD : BLOCK_ROWS, :].bitcast(I32),
+            )
+        n1_t = load_list(n1, "n1_t")
+        w2_raw = keep.tile([P, PACK, H], F32, name="w2_raw", tag="raw_b")
+        load_columns(w2_raw, w2, HALF, H)
+        load_columns(w2_raw, w2, 0, HALF)
+
+        y_pl = planes_with_spare("y_pl", "y_pl")
+        u_pl = planes_with_spare("u_pl", "u_pl")
+        d_win = [window_tile("d_win%d" % t) for t in range(PACK)]
+        h_win = [window_tile("h_win%d" % t) for t in range(PACK)]
+
+        w1_op = operand("w1", H, "w1_bf", "w1_codes")
+        w2_op = operand("w2", H, "w2_bf", "w2_codes")
+        round_dealt(round_on_scalar, w1_op, w1_raw, 0, HALF)
+        round_dealt(round_on_vector, w1_op, w1_raw, HALF, H)
+        n2_t = load_list(n2, "n2_t")
+        w3_raw = keep.tile([P, PACK, H], F32, name="w3_raw", tag="raw_a")
+        load_columns(w3_raw, w3, HALF, H)
+        load_columns(w3_raw, w3, 0, HALF)
+        quantize(w1_op)
+
+        picked_words = keep.tile([P, 2 * S], U32, name="picked_words", tag="w1_bf", align_bytes=64)
+        nc.vector.tensor_copy(picked_words[:, :S], word_table[:].bitcast(U32).indirect(offs_t[:]))
+        y_bank = {}
+        for t in order:
+            y_bank[t] = psum.tile([P, S], F32, name="y_bank%d" % t, tag="bank_a%d" % t)
+            product(y_bank[t], w1_op, t, picked_words[:, :S], x_scale_rows[:, :S], True, True)
+        nc.vector.tensor_copy(picked_words[:, S:], word_table[:].bitcast(U32).indirect(hz_t[:]))
+
+        gn_t = load_dealt_rows(gn, "gn_t")
+        n3_t = load_list(n3, "n3_t")
+        tau_t = load_dealt_rows(tau, "tau_t")
+        n4_t = load_list(n4, "n4_t")
+        w4_raw = keep.tile([P, PACK, H], F32, name="w4_raw", tag="raw_c")
+        load_columns(w4_raw, w4, 0, H)
+        gm_t = load_dealt_rows(gm, "gm_t")
+        n5_t = load_list(n5, "n5_t")
+        n6_t = load_list(n6, "n6_t")
+        tau2_t = keep.tile([P, PACK], F32, name="tau2_t")
+        with nc.allow_non_contiguous_dma(reason="one rate a row of h: row 128 t + p lands at [p, t]"):
+            nc.sync.dma_start(tau2_t[:], tau2.rearrange("(t p) o -> p (t o)", p=P))
 
         for t in order:
-            nc.scalar.activation(plane(g3, t), plane_window(u_pl, t).indirect(n3_t[:]), ACT.Copy, scale=0.5)
+            nc.scalar.copy(plane(y_pl, t), y_bank[t][:])
+
+        round_dealt(round_on_vector, w2_op, w2_raw, HALF, H)
+        round_dealt(round_on_vector, w2_op, w2_raw, 0, HALF)
+        quantize(w2_op)
+        d_bank = {}
+        for t in order:
+            d_bank[t] = psum.tile([P, S], F32, name="d_bank%d" % t, tag="bank_b%d" % t)
+            product(d_bank[t], w2_op, t, picked_words[:, S:], x_scale_rows[:, S:], True, True)
+
+        pair = PACK // 2
+        first_two, last_two = order[:pair], order[pair:]
+        upper = operand("upper", PACK * P, "upper_bf", "upper_codes")
+        for b, t in enumerate(first_two):
+            round_block(round_on_vector, upper, b, w3_raw, t)
+
+        st_pl = planes_with_spare("st_pl", "raw_b")
+        y_n1 = keep.tile([P, PACK * S], F32, name="y_n1")
+        st_n2 = keep.tile([P, PACK * S], F32, name="st_n2")
+        half_u_n3 = keep.tile([P, PACK * S], F32, name="half_u_n3", tag="half_u_n3", align_bytes=64)
+        su = keep.tile([P, PACK * S], F32, name="su")
+        for t in order:
+            nc.scalar.activation(plane(y_n1, t), plane_window(y_pl, t).indirect(n1_t[:]), ACT.Copy)
+        for t in order:
+            nc.vector.tensor_tensor(plane(st_pl, t), y_bank[t][:], plane(y_n1, t), ALU.subtract)
+
+        top = keep.tile([P, PACK], F32, name="top", tag="top", align_bytes=64)
+        bias = keep.tile([P, PACK], F32, name="bias", tag="bias", align_bytes=64)
+        ea = keep.tile([P, PACK * S], F32, name="ea")
+        dg = keep.tile([P, PACK * S], F32, name="dg", tag="dg", align_bytes=64)
         for t in order:
             col = slice(t, t + 1)
-            nc.scalar.activation(plane(ea, t), d_win[t][:].indirect(n4_t[:]), ACT.Exp, bias=bias[:, col], scale=tau_t[:, col])
-        nc.vector.tensor_tensor(packed(z_bf), woven(u_pl), woven(g3), ALU.add)
-        nc.vector.quantize_mx(out=z_codes[:].bitcast(FP8X4), scales=z_scales[:], in_=z_bf[:])
-        h_bank = {}
+            nc.scalar.activation(plane(st_n2, t), plane_window(st_pl, t).indirect(n2_t[:]), ACT.Copy)
+            nc.vector.tensor_tensor(plane(su, t), plane(st_pl, t), plane(st_n2, t), ALU.max)
+            nc.vector.tensor_scalar(d_win[t][:, :S], d_bank[t][:], 1.0, None, ALU.mult, ALU.max, accum_out=top[:, col])
+            nc.vector.tensor_scalar(plane(u_pl, t), plane(su, t), gn_t[:, col], None, ALU.mult)
+        nc.vector.scalar_tensor_tensor(bias[:], top[:], -1.0, tau_t[:], ALU.mult, ALU.mult)
+
+        for b, t in enumerate(first_two):
+            round_block(round_on_vector, upper, pair + b, w4_raw, t)
+        quantize(upper)
+
         for t in order:
-            h_bank[t] = psum.tile([P, S], F32, name="h_bank%d" % t, tag="a%d" % t)
-            product(h_bank[t], wt3, t, z_codes, z_scales, True, False)
-        nc.vector.tensor_tensor(packed(z2_bf), woven(dg), woven(ea), ALU.mult)
-        nc.vector.quantize_mx(out=z2_codes[:].bitcast(FP8X4), scales=z2_scales[:], in_=z2_bf[:])
+            nc.scalar.activation(plane(half_u_n3, t), plane_window(u_pl, t).indirect(n3_t[:]), ACT.Copy, scale=0.5)
+        for t in order:
+            col = slice(t, t + 1)
+            nc.scalar.activation(
+                plane(ea, t), d_win[t][:].indirect(n4_t[:]), ACT.Exp, bias=bias[:, col], scale=tau_t[:, col]
+            )
+
+        z_op = operand("z", S, "upper_bf", "z_codes")
+        nc.vector.tensor_tensor(packed(z_op[0]), woven(u_pl), woven(half_u_n3), ALU.add)
+        quantize(z_op)
+        for t in order:
+            nc.vector.tensor_scalar(plane(dg, t), d_win[t][:, :S], gm_t[:, t : t + 1], 2.0, ALU.mult, ALU.mult)
+        z2_op = operand("z2", S, "half_u_n3", "z2_codes")
+        nc.vector.tensor_tensor(packed(z2_op[0]), woven(dg), woven(ea), ALU.mult)
+
+        lower = {}
+        for t, tag, codes_tag in zip(last_two, ("top", "bias"), ("dg", "half_u_n3")):
+            lower[t] = operand("lower%d" % t, 2 * P, tag, codes_tag)
+            round_block(round_on_scalar, lower[t], 0, w3_raw, t)
+            round_block(round_on_scalar, lower[t], 1, w4_raw, t)
+        quantize(z2_op)
+        quantize(lower[last_two[0]])
 
         top2 = keep.tile([P, PACK], F32, name="top2")
         bias2 = keep.tile([P, PACK], F32, name="bias2")
         ea2 = [keep.tile([P, S], F32, name="ea2_%d" % t) for t in range(PACK)]
-        g6 = [keep.tile([P, S], F32, name="g6_%d" % t) for t in range(PACK)]
+        h_n6 = [keep.tile([P, S], F32, name="h_n6_%d" % t) for t in range(PACK)]
+        h_bank = {}
+
+        def sum_products(t, op, w3_block, w4_block):
+            h_bank[t] = psum.tile([P, S], F32, name="h_bank%d" % t, tag="bank_a%d" % t)
+            product(h_bank[t], op, w3_block, z_op[1][:], z_op[2][:], True, False)
+            product(h_bank[t], op, w4_block, z2_op[1][:], z2_op[2][:], False, True)
+
+        def leave_psum(t):
+            col = slice(t, t + 1)
+            nc.vector.tensor_scalar(h_win[t][:, :S], h_bank[t][:], 1.0, None, ALU.mult, ALU.max, accum_out=top2[:, col])
+            nc.vector.tensor_scalar(bias2[:, col], top2[:, col], tau2_t[:, col], -1.0, ALU.mult, ALU.mult)
+
+        for b, t in enumerate(first_two):
+            sum_products(t, upper, b, pair + b)
+        leave_psum(first_two[0])
+        quantize(lower[last_two[1]])
+        leave_psum(first_two[1])
+        for t in last_two:
+            sum_products(t, lower[t], 0, 1)
+        for t in last_two:
+            leave_psum(t)
+
         for t in order:
             col = slice(t, t + 1)
-            cast_plain("scalar", wt4, w4_raw, t)
-            quantize(wt4, t, t + 1)
-            product(h_bank[t], wt4, t, z2_codes, z2_scales, False, True)
-            nc.vector.tensor_scalar(h_win[t][:, :S], h_bank[t][:], 1.0, None, ALU.mult, ALU.max, accum_out=top2[:, col])
-            nc.gpsimd.tensor_scalar(bias2[:, col], top2[:, col], tau2_t[:, col], -1.0, ALU.mult, ALU.mult)
-
-        def fetch(t):
-            nc.scalar.activation(g6[t][:], h_win[t][:].indirect(n6_t[:]), ACT.Copy)
-
-        def expo(t):
-            col = slice(t, t + 1)
-            nc.scalar.activation(ea2[t][:], h_win[t][:].indirect(n5_t[:]), ACT.Exp, bias=bias2[:, col], scale=tau2_t[:, col])
-
-        def finish(t):
-            big = keep.tile([P, S], F32, name="big_%d" % t)
-            res = keep.tile([P, S], F32, name="res_%d" % t)
-            nc.vector.scalar_tensor_tensor(big[:], ea2[t][:], 2.0, h_bank[t][:], ALU.mult, ALU.max)
-            nc.vector.scalar_tensor_tensor(res[:], g6[t][:], -0.5, big[:], ALU.mult, ALU.add)
-            nc.sync.dma_start(out[P * t : P * (t + 1), :], res[:])
-
-        nc.vector.tensor_copy(g6[0][:], h_win[0][:].indirect(n6_t[:]))
-        fetch(3)
-        expo(3)
-        expo(2)
-        fetch(2)
-        expo(1)
-        expo(0)
-        fetch(1)
-        for t in (3, 2, 0, 1):
-            finish(t)
+            nc.scalar.activation(
+                ea2[t][:], h_win[t][:].indirect(n5_t[:]), ACT.Exp, bias=bias2[:, col], scale=tau2_t[:, col]
+            )
+            if t % 2 == 0:
+                nc.vector.tensor_copy(h_n6[t][:], h_win[t][:].indirect(n6_t[:]))
+            else:
+                nc.scalar.activation(h_n6[t][:], h_win[t][:].indirect(n6_t[:]), ACT.Copy, scale=-0.5)
+        for t in order:
+            larger = keep.tile([P, S], F32, name="larger_%d" % t)
+            result = keep.tile([P, S], F32, name="result_%d" % t)
+            nc.vector.scalar_tensor_tensor(larger[:], ea2[t][:], 2.0, h_bank[t][:], ALU.mult, ALU.max)
+            if t % 2 == 0:
+                nc.vector.scalar_tensor_tensor(result[:], h_n6[t][:], -0.5, larger[:], ALU.mult, ALU.add)
+            else:
+                nc.gpsimd.tensor_tensor(result[:], h_n6[t][:], larger[:], ALU.add)
+            nc.sync.dma_start(out[P * t : P * (t + 1), :], result[:])

from contextlib import ExitStack

import concourse.mybir as mybir

F32 = mybir.dt.float32
BF16 = mybir.dt.bfloat16
I32 = mybir.dt.int32
U32 = mybir.dt.uint32
U16 = mybir.dt.uint16
U8 = mybir.dt.uint8
FP8X4 = mybir.dt.float8_e4m3fn_x4
ALU = mybir.AluOpType
ACT = mybir.ActivationFunctionType

P = 128
PACK = 4
T = 2048
S = 256
H = 512
HALF = H // 2
WIN = 2 * S
LINE = 4
GROUP = 16
QUAD = 32
BLOCK_ROWS = 8

FLOPS = 2 * 4 * 512 * 512 * 256


def tile_picked_hjointhreeepkecl_none_p_kernel(
    tc, x_words, x_scales, w1, w2, tau, gn, gm, w3, w4, tau2, offs, hz, n1, n2, n3, n4, n5, n6, out
):
    nc = tc.nc
    with ExitStack() as ctx:
        keep = ctx.enter_context(tc.tile_pool(name="keep", bufs=1))
        psum = ctx.enter_context(tc.psum_pool(name="psum", bufs=1))

        def load_list(src, name):
            lst = keep.tile([P, S // GROUP], U16, name=name)
            nc.sync.dma_start(lst[:], src)
            return lst

        def load_dealt_rows(src, name):
            vec = keep.tile([P, PACK], F32, name=name)
            nc.sync.dma_start(vec[:], src.rearrange("(p t) o -> p (t o)", t=PACK))
            return vec

        def load_columns(raw, src, c0, c1):
            nc.sync.dma_start(raw[:, :, c0:c1], src.rearrange("(p j) c -> p j c", j=PACK)[:, :, c0:c1])

        def operand(name, width, tag, codes_tag):
            return (
                keep.tile([P, PACK * width], BF16, name=name + "_bf", tag=tag, align_bytes=64),
                keep.tile([P, width], U32, name=name + "_codes", tag=codes_tag, align_bytes=64),
                keep.tile([P, width], U8, name=name + "_scales", align_bytes=64),
            )

        def round_on_vector(dst, src):
            nc.vector.tensor_copy(dst, src)

        def round_on_scalar(dst, src):
            nc.scalar.activation(dst, src, ACT.Copy)

        def round_dealt(rounder, op, raw, c0, c1):
            dst = op[0][:].rearrange("p (t m j) -> p m j t", t=PACK, j=PACK)[:, c0 // PACK : c1 // PACK]
            rounder(dst, raw[:, :, c0:c1].rearrange("p j (m t) -> p m j t", t=PACK))

        def round_block(rounder, op, b, raw, t):
            dst = op[0][:, PACK * P * b : PACK * P * (b + 1)].rearrange("p (c a j) -> p c j a", a=LINE, j=PACK)
            rounder(dst, raw[:, :, P * t : P * (t + 1)].rearrange("p j (c a) -> p c j a", a=LINE))

        def quantize(op):
            nc.vector.quantize_mx(out=op[1][:].bitcast(FP8X4), scales=op[2][:], in_=op[0][:])

        def product(bank, op, b, codes, scales, start, stop):
            cols = slice(P * b, P * (b + 1))
            nc.tensor.matmul_mx(
                out=bank[:], lhsT=op[1][:, cols].bitcast(FP8X4), lhsT_scale=op[2][:, cols],
                rhs=codes.bitcast(FP8X4), rhs_scale=scales, start=start, stop=stop,
            )

        def planes_with_spare(name, tag):
            tile = keep.tile([P, (PACK + 1) * S], F32, name=name, tag=tag)
            nc.vector.memset(tile[:, PACK * S :], 0.0)
            return tile

        def window_tile(name):
            tile = keep.tile([P, WIN], F32, name=name)
            nc.vector.memset(tile[:, S:], 0.0)
            return tile

        def plane(tile, t):
            return tile[:, S * t : S * (t + 1)]

        def plane_window(tile, t):
            return tile[:, S * t : S * t + WIN]

        def woven(tile):
            return tile[:, : PACK * S].rearrange("p (t c a) -> p c t a", t=PACK, a=LINE)

        def packed(tile):
            return tile[:].rearrange("p (c a t) -> p c t a", t=PACK, a=LINE)

        order = list(reversed(range(PACK)))

        scale_table = keep.tile([P, T], U8, name="scale_table", tag="raw_b")
        nc.gpsimd.memset(scale_table[:].bitcast(I32), 0)
        w1_raw = keep.tile([P, PACK, H], F32, name="w1_raw", tag="raw_a")
        load_columns(w1_raw, w1, 0, HALF)
        offs_t = load_list(offs, "offs_t")
        hz_t = load_list(hz, "hz_t")
        nc.sync.dma_start(scale_table[0:P:BLOCK_ROWS, :].bitcast(I32), x_scales[0].bitcast(I32))
        load_columns(w1_raw, w1, HALF, H)
        word_table = keep.tile([P, T], I32, name="word_table", tag="raw_c")
        nc.sync.dma_start(word_table[:], x_words[0].rearrange("p c j -> p (c j)").bitcast(I32))

        picked_scales = keep.tile([P, 2 * S], U8, name="picked_scales")
        x_scale_rows = keep.tile([P, 2 * S], U8, name="x_scale_rows", align_bytes=64)
        nc.vector.memset(x_scale_rows[:].bitcast(I32), 0)
        nc.vector.tensor_copy(picked_scales[:, :S], scale_table[:].indirect(offs_t[:]))
        nc.vector.tensor_copy(picked_scales[:, S:], scale_table[:].indirect(hz_t[:]))
        for q0 in range(0, P, QUAD):
            nc.sync.dma_start(
                x_scale_rows[q0 : q0 + QUAD // BLOCK_ROWS, :].bitcast(I32),
                picked_scales[q0 : q0 + QUAD : BLOCK_ROWS, :].bitcast(I32),
            )
        n1_t = load_list(n1, "n1_t")
        w2_raw = keep.tile([P, PACK, H], F32, name="w2_raw", tag="raw_b")
        load_columns(w2_raw, w2, HALF, H)
        load_columns(w2_raw, w2, 0, HALF)

        y_pl = planes_with_spare("y_pl", "y_pl")
        u_pl = planes_with_spare("u_pl", "u_pl")
        d_win = [window_tile("d_win%d" % t) for t in range(PACK)]
        h_win = [window_tile("h_win%d" % t) for t in range(PACK)]

        w1_op = operand("w1", H, "w1_bf", "w1_codes")
        w2_op = operand("w2", H, "w2_bf", "w2_codes")
        round_dealt(round_on_scalar, w1_op, w1_raw, 0, HALF)
        round_dealt(round_on_vector, w1_op, w1_raw, HALF, H)
        n2_t = load_list(n2, "n2_t")
        w3_raw = keep.tile([P, PACK, H], F32, name="w3_raw", tag="raw_a")
        load_columns(w3_raw, w3, HALF, H)
        load_columns(w3_raw, w3, 0, HALF)
        quantize(w1_op)

        picked_words = keep.tile([P, 2 * S], U32, name="picked_words", tag="w1_bf", align_bytes=64)
        nc.vector.tensor_copy(picked_words[:, :S], word_table[:].bitcast(U32).indirect(offs_t[:]))
        y_bank = {}
        for t in order:
            y_bank[t] = psum.tile([P, S], F32, name="y_bank%d" % t, tag="bank_a%d" % t)
            product(y_bank[t], w1_op, t, picked_words[:, :S], x_scale_rows[:, :S], True, True)
        nc.vector.tensor_copy(picked_words[:, S:], word_table[:].bitcast(U32).indirect(hz_t[:]))

        gn_t = load_dealt_rows(gn, "gn_t")
        n3_t = load_list(n3, "n3_t")
        tau_t = load_dealt_rows(tau, "tau_t")
        n4_t = load_list(n4, "n4_t")
        w4_raw = keep.tile([P, PACK, H], F32, name="w4_raw", tag="raw_c")
        load_columns(w4_raw, w4, 0, H)
        gm_t = load_dealt_rows(gm, "gm_t")
        n5_t = load_list(n5, "n5_t")
        n6_t = load_list(n6, "n6_t")
        tau2_t = keep.tile([P, PACK], F32, name="tau2_t")
        with nc.allow_non_contiguous_dma(reason="one rate a row of h: row 128 t + p lands at [p, t]"):
            nc.sync.dma_start(tau2_t[:], tau2.rearrange("(t p) o -> p (t o)", p=P))

        for t in order:
            nc.scalar.copy(plane(y_pl, t), y_bank[t][:])

        round_dealt(round_on_vector, w2_op, w2_raw, HALF, H)
        round_dealt(round_on_vector, w2_op, w2_raw, 0, HALF)
        quantize(w2_op)
        d_bank = {}
        for t in order:
            d_bank[t] = psum.tile([P, S], F32, name="d_bank%d" % t, tag="bank_b%d" % t)
            product(d_bank[t], w2_op, t, picked_words[:, S:], x_scale_rows[:, S:], True, True)

        pair = PACK // 2
        first_two, last_two = order[:pair], order[pair:]
        upper = operand("upper", PACK * P, "upper_bf", "upper_codes")
        for b, t in enumerate(first_two):
            round_block(round_on_vector, upper, b, w3_raw, t)

        st_pl = planes_with_spare("st_pl", "raw_b")
        y_n1 = keep.tile([P, PACK * S], F32, name="y_n1")
        st_n2 = keep.tile([P, PACK * S], F32, name="st_n2")
        half_u_n3 = keep.tile([P, PACK * S], F32, name="half_u_n3", tag="half_u_n3", align_bytes=64)
        su = keep.tile([P, PACK * S], F32, name="su")
        for t in order:
            nc.scalar.activation(plane(y_n1, t), plane_window(y_pl, t).indirect(n1_t[:]), ACT.Copy)
        for t in order:
            nc.vector.tensor_tensor(plane(st_pl, t), y_bank[t][:], plane(y_n1, t), ALU.subtract)

        top = keep.tile([P, PACK], F32, name="top", tag="top", align_bytes=64)
        bias = keep.tile([P, PACK], F32, name="bias", tag="bias", align_bytes=64)
        ea = keep.tile([P, PACK * S], F32, name="ea")
        dg = keep.tile([P, PACK * S], F32, name="dg", tag="dg", align_bytes=64)
        for t in order:
            col = slice(t, t + 1)
            nc.scalar.activation(plane(st_n2, t), plane_window(st_pl, t).indirect(n2_t[:]), ACT.Copy)
            nc.vector.tensor_tensor(plane(su, t), plane(st_pl, t), plane(st_n2, t), ALU.max)
            nc.vector.tensor_scalar(d_win[t][:, :S], d_bank[t][:], 1.0, None, ALU.mult, ALU.max, accum_out=top[:, col])
            nc.vector.tensor_scalar(plane(u_pl, t), plane(su, t), gn_t[:, col], None, ALU.mult)
        nc.vector.scalar_tensor_tensor(bias[:], top[:], -1.0, tau_t[:], ALU.mult, ALU.mult)

        for b, t in enumerate(first_two):
            round_block(round_on_vector, upper, pair + b, w4_raw, t)
        quantize(upper)

        for t in order:
            nc.scalar.activation(plane(half_u_n3, t), plane_window(u_pl, t).indirect(n3_t[:]), ACT.Copy, scale=0.5)
        for t in order:
            col = slice(t, t + 1)
            nc.scalar.activation(
                plane(ea, t), d_win[t][:].indirect(n4_t[:]), ACT.Exp, bias=bias[:, col], scale=tau_t[:, col]
            )

        z_op = operand("z", S, "upper_bf", "z_codes")
        nc.vector.tensor_tensor(packed(z_op[0]), woven(u_pl), woven(half_u_n3), ALU.add)
        quantize(z_op)
        for t in order:
            nc.vector.tensor_scalar(plane(dg, t), d_win[t][:, :S], gm_t[:, t : t + 1], 2.0, ALU.mult, ALU.mult)
        z2_op = operand("z2", S, "half_u_n3", "z2_codes")
        nc.vector.tensor_tensor(packed(z2_op[0]), woven(dg), woven(ea), ALU.mult)

        lower = {}
        for t, tag, codes_tag in zip(last_two, ("top", "bias"), ("dg", "half_u_n3")):
            lower[t] = operand("lower%d" % t, 2 * P, tag, codes_tag)
            round_block(round_on_scalar, lower[t], 0, w3_raw, t)
            round_block(round_on_scalar, lower[t], 1, w4_raw, t)
        quantize(z2_op)
        quantize(lower[last_two[0]])

        top2 = keep.tile([P, PACK], F32, name="top2")
        bias2 = keep.tile([P, PACK], F32, name="bias2")
        ea2 = [keep.tile([P, S], F32, name="ea2_%d" % t) for t in range(PACK)]
        h_n6 = [keep.tile([P, S], F32, name="h_n6_%d" % t) for t in range(PACK)]
        h_bank = {}

        def sum_products(t, op, w3_block, w4_block):
            h_bank[t] = psum.tile([P, S], F32, name="h_bank%d" % t, tag="bank_a%d" % t)
            product(h_bank[t], op, w3_block, z_op[1][:], z_op[2][:], True, False)
            product(h_bank[t], op, w4_block, z2_op[1][:], z2_op[2][:], False, True)

        def leave_psum(t):
            col = slice(t, t + 1)
            nc.vector.tensor_scalar(h_win[t][:, :S], h_bank[t][:], 1.0, None, ALU.mult, ALU.max, accum_out=top2[:, col])
            nc.vector.tensor_scalar(bias2[:, col], top2[:, col], tau2_t[:, col], -1.0, ALU.mult, ALU.mult)

        for b, t in enumerate(first_two):
            sum_products(t, upper, b, pair + b)
        leave_psum(first_two[0])
        quantize(lower[last_two[1]])
        leave_psum(first_two[1])
        for t in last_two:
            sum_products(t, lower[t], 0, 1)
        for t in last_two:
            leave_psum(t)

        for t in order:
            col = slice(t, t + 1)
            nc.scalar.activation(
                ea2[t][:], h_win[t][:].indirect(n5_t[:]), ACT.Exp, bias=bias2[:, col], scale=tau2_t[:, col]
            )
            if t % 2 == 0:
                nc.vector.tensor_copy(h_n6[t][:], h_win[t][:].indirect(n6_t[:]))
            else:
                nc.scalar.activation(h_n6[t][:], h_win[t][:].indirect(n6_t[:]), ACT.Copy, scale=-0.5)
        for t in order:
            larger = keep.tile([P, S], F32, name="larger_%d" % t)
            result = keep.tile([P, S], F32, name="result_%d" % t)
            nc.vector.scalar_tensor_tensor(larger[:], ea2[t][:], 2.0, h_bank[t][:], ALU.mult, ALU.max)
            if t % 2 == 0:
                nc.vector.scalar_tensor_tensor(result[:], h_n6[t][:], -0.5, larger[:], ALU.mult, ALU.add)
            else:
                nc.gpsimd.tensor_tensor(result[:], h_n6[t][:], larger[:], ALU.add)
            nc.sync.dma_start(out[P * t : P * (t + 1), :], result[:])
